import numpy as np
CORES = [4,5,6,7,12,13,14,15,132,133,134,135,140,141,142,143]
N = 16
ROWS, COLS = 2, 8
def setup_inputs(rng):
    return {"x": rng.standard_normal((N, 128, 128), dtype=np.float32)}
def reference(x):
    g = x.astype(np.float64).reshape(ROWS, COLS, 128, 128)
    rs = g.sum(axis=1)
    cs = g.sum(axis=0)
    y1 = np.stack([rs[r // COLS] for r in range(N)]).astype(x.dtype)
    y2 = np.stack([cs[r % COLS] for r in range(N)]).astype(x.dtype)
    return {"y1": y1, "y2": y2}

@@ -1,0 +1,69 @@
+from concourse.bass import DstId, RemoteDMATransfer
+from concourse.mybir import AluOpType
+
+SCRATCH = {
+    "S": ("dram", [2, 128, 64], "float32"),
+    "X": ("dram", [4, 128, 64], "float32"),
+    "P": ("dram", [128, 64], "float32"),
+    "L1": ("dram", [2, 128, 64], "float32"),
+    "L2": ("dram", [2, 128, 64], "float32"),
+}
+SEMAPHORES = ["ld", "c2", "st", "a2", "snt", "xa", "pp", "ta", "pa"]
+
+
+def rank_program(g, core, T, topo):
+    c = core % 8
+    if topo.chip(core) > 1:
+        return
+    base = core - c
+    sem = T.sem
+
+    def dst(d):
+        rid, pid = topo.addr(d, core)
+        return DstId(rid=rid, pnc=pid)
+
+    rank = T.rank_of(core)
+    if rank is not None:
+        k = c - 4
+        partner = T.cores[(rank + 8) % 16]
+        g.sync.dma_start(T.S[:], T.x[:]).then_inc(sem.ld, 16)
+        g.sync.dma_start(T.y2[:], T.x[:]).then_inc(sem.c2, 16)
+        g.wait_ge(sem.ld, 16)
+        g.remote_dma_fused([
+            RemoteDMATransfer(dst_ids=[dst(base + 2)], dma_engine_mask=0x00FF, remote_sem=sem.xa,
+                              src=T.S[0], dst=T.X[k]),
+            RemoteDMATransfer(dst_ids=[dst(base + 3)], dma_engine_mask=0xFF00, remote_sem=sem.xa,
+                              src=T.S[1], dst=T.X[k]),
+        ], local_sem=sem.snt)
+        g.remote_dma_fused([
+            RemoteDMATransfer(dst_ids=[dst(partner)], dma_engine_mask=0x000F, remote_sem=sem.pa,
+                              src=T.S[0], dst=T.L2[0]),
+            RemoteDMATransfer(dst_ids=[dst(partner)], dma_engine_mask=0x00F0, remote_sem=sem.pa,
+                              src=T.S[1], dst=T.L2[1]),
+        ], local_sem=sem.snt)
+        g.sync.wait_ge(sem.ta, 32)
+        g.sync.dma_start(T.y1[:], T.L1[:]).then_inc(sem.st, 16)
+        g.wait_ge(sem.pa, 8)
+        g.wait_ge(sem.c2, 16)
+        g.dma_start(T.y2[:], T.L2[:], accum_op=AluOpType.add, max_dma_last_dim=8192).then_inc(sem.a2, 16)
+        g.wait_ge(sem.snt, 24)
+        g.wait_ge(sem.a2, 16)
+        g.wait_ge(sem.ta, 32)
+        g.wait_ge(sem.st, 16)
+        return
+
+    if c in (2, 3):
+        h = c - 2
+        peer = core ^ 8
+        slots = [T.X[j] for j in range(4)]
+        g.wait_ge(sem.xa, 32)
+        g.remote_dma_fused([
+            RemoteDMATransfer(dst_ids=[dst(peer)], dma_engine_mask=0x00FF, remote_sem=sem.pp,
+                              srcs=slots, dsts=[T.P[:]], alu_op=1),
+        ], local_sem=sem.snt)
+        g.wait_ge(sem.pp, 8)
+        g.remote_dma_fused([
+            RemoteDMATransfer(dst_ids=[dst(base + 4 + j) for j in range(4)], dma_engine_mask=0xFFFF, remote_sem=sem.ta,
+                              srcs=slots + [T.P[:]], dsts=[T.L1[h]] * 4, alu_op=1),
+        ], local_sem=sem.snt)
+        g.wait_ge(sem.snt, 24)

@@ -1,14 +1,21 @@
 from concourse.bass import DstId, RemoteDMATransfer
 from concourse.mybir import AluOpType
 
+RED = [2, 3, 6, 7]
+NP = len(RED)
+W = 128 // NP
 SCRATCH = {
-    "S": ("dram", [2, 128, 64], "float32"),
-    "X": ("dram", [4, 128, 64], "float32"),
-    "P": ("dram", [128, 64], "float32"),
-    "L1": ("dram", [2, 128, 64], "float32"),
-    "L2": ("dram", [2, 128, 64], "float32"),
+    "S": ("dram", [NP, 128, W], "float32"),
+    "X": ("dram", [4, 128, W], "float32"),
+    "P": ("dram", [128, W], "float32"),
+    "L1": ("dram", [NP, 128, W], "float32"),
+    "L2": ("dram", [NP, 128, W], "float32"),
 }
 SEMAPHORES = ["ld", "c2", "st", "a2", "snt", "xa", "pp", "ta", "pa"]
+
+
+def group(p, n, lo):
+    return ((1 << n) - 1) << (lo + p * n)
 
 
 def rank_program(g, core, T, topo):
@@ -17,53 +24,70 @@ def rank_program(g, core, T, topo):
         return
     base = core - c
     sem = T.sem
+    sent = [0]
 
     def dst(d):
         rid, pid = topo.addr(d, core)
         return DstId(rid=rid, pnc=pid)
 
+    def call(transfers, engines):
+        g.remote_dma_fused(transfers, local_sem=sem.snt)
+        sent[0] += engines
+
+    def reduce_piece(p, own, between):
+        peer = core ^ 8
+        if own is None:
+            srcs = [T.X[j] for j in range(4)]
+        else:
+            srcs = [own] + [T.X[j] for j in range(4) if j != c - 4]
+        g.wait_ge(sem.xa, (16 // NP) * (4 if own is None else 3))
+        call([RemoteDMATransfer(dst_ids=[dst(peer)], dma_engine_mask=0x00FF, remote_sem=sem.pp,
+                                srcs=srcs, dsts=[T.P[:]], alu_op=1)], 8)
+        if between is not None:
+            between()
+        g.wait_ge(sem.pp, 8)
+        srcs = srcs + [T.P[:]]
+        if own is None:
+            call([RemoteDMATransfer(dst_ids=[dst(base + 4 + j) for j in range(4)], dma_engine_mask=0xFFFF,
+                                    remote_sem=sem.ta, srcs=srcs, dsts=[T.L1[p]] * 4, alu_op=1)], 16)
+        else:
+            others = [base + 4 + j for j in range(4) if j != c - 4]
+            call([RemoteDMATransfer(dst_ids=[dst(d) for d in others], dma_engine_mask=0xFF00,
+                                    remote_sem=sem.ta, srcs=srcs, dsts=[T.L1[p]] * 3, alu_op=1),
+                  RemoteDMATransfer(dst_ids=[dst(peer)], dma_engine_mask=0x00FF,
+                                    remote_sem=sem.ta, srcs=srcs, dsts=[T.L1[p]], alu_op=1)], 16)
+
     rank = T.rank_of(core)
     if rank is not None:
         k = c - 4
         partner = T.cores[(rank + 8) % 16]
+        total = sum(16 if rc < 4 else 8 for rc in RED)
         g.sync.dma_start(T.S[:], T.x[:]).then_inc(sem.ld, 16)
         g.sync.dma_start(T.y2[:], T.x[:]).then_inc(sem.c2, 16)
         g.wait_ge(sem.ld, 16)
-        g.remote_dma_fused([
-            RemoteDMATransfer(dst_ids=[dst(base + 2)], dma_engine_mask=0x00FF, remote_sem=sem.xa,
-                              src=T.S[0], dst=T.X[k]),
-            RemoteDMATransfer(dst_ids=[dst(base + 3)], dma_engine_mask=0xFF00, remote_sem=sem.xa,
-                              src=T.S[1], dst=T.X[k]),
-        ], local_sem=sem.snt)
-        g.remote_dma_fused([
-            RemoteDMATransfer(dst_ids=[dst(partner)], dma_engine_mask=0x000F, remote_sem=sem.pa,
-                              src=T.S[0], dst=T.L2[0]),
-            RemoteDMATransfer(dst_ids=[dst(partner)], dma_engine_mask=0x00F0, remote_sem=sem.pa,
-                              src=T.S[1], dst=T.L2[1]),
-        ], local_sem=sem.snt)
-        g.sync.wait_ge(sem.ta, 32)
+        tr = [RemoteDMATransfer(dst_ids=[dst(base + rc)], dma_engine_mask=group(p, 16 // NP, 0), remote_sem=sem.xa,
+                                src=T.S[p], dst=T.X[k]) for p, rc in enumerate(RED) if rc != c]
+        call(tr, (16 // NP) * len(tr))
+
+        def send_y2():
+            call([RemoteDMATransfer(dst_ids=[dst(partner)], dma_engine_mask=group(p, 8 // NP, 0), remote_sem=sem.pa,
+                                    src=T.S[p], dst=T.L2[p]) for p in range(NP)], 8)
+
+        g.sync.wait_ge(sem.ta, total)
         g.sync.dma_start(T.y1[:], T.L1[:]).then_inc(sem.st, 16)
+        if c in RED:
+            reduce_piece(RED.index(c), T.S[RED.index(c)], send_y2)
+        else:
+            send_y2()
         g.wait_ge(sem.pa, 8)
         g.wait_ge(sem.c2, 16)
         g.dma_start(T.y2[:], T.L2[:], accum_op=AluOpType.add, max_dma_last_dim=8192).then_inc(sem.a2, 16)
-        g.wait_ge(sem.snt, 24)
+        g.wait_ge(sem.snt, sent[0])
         g.wait_ge(sem.a2, 16)
-        g.wait_ge(sem.ta, 32)
+        g.wait_ge(sem.ta, total)
         g.wait_ge(sem.st, 16)
         return
 
-    if c in (2, 3):
-        h = c - 2
-        peer = core ^ 8
-        slots = [T.X[j] for j in range(4)]
-        g.wait_ge(sem.xa, 32)
-        g.remote_dma_fused([
-            RemoteDMATransfer(dst_ids=[dst(peer)], dma_engine_mask=0x00FF, remote_sem=sem.pp,
-                              srcs=slots, dsts=[T.P[:]], alu_op=1),
-        ], local_sem=sem.snt)
-        g.wait_ge(sem.pp, 8)
-        g.remote_dma_fused([
-            RemoteDMATransfer(dst_ids=[dst(base + 4 + j) for j in range(4)], dma_engine_mask=0xFFFF, remote_sem=sem.ta,
-                              srcs=slots + [T.P[:]], dsts=[T.L1[h]] * 4, alu_op=1),
-        ], local_sem=sem.snt)
-        g.wait_ge(sem.snt, 24)
+    if c in RED:
+        reduce_piece(RED.index(c), None, None)
+        g.wait_ge(sem.snt, sent[0])

@@ -2,8 +2,8 @@ from concourse.bass import DstId, RemoteDMATransfer
 from concourse.mybir import AluOpType
 
 RED = [2, 3, 6, 7]
-NP = len(RED)
-W = 128 // NP
+NP = 4
+W = 32
 SCRATCH = {
     "S": ("dram", [NP, 128, W], "float32"),
     "X": ("dram", [4, 128, W], "float32"),
@@ -14,8 +14,8 @@ SCRATCH = {
 SEMAPHORES = ["ld", "c2", "st", "a2", "snt", "xa", "pp", "ta", "pa"]
 
 
-def group(p, n, lo):
-    return ((1 << n) - 1) << (lo + p * n)
+def group(p, n):
+    return ((1 << n) - 1) << (p * n)
 
 
 def rank_program(g, core, T, topo):
@@ -40,7 +40,7 @@ def rank_program(g, core, T, topo):
             srcs = [T.X[j] for j in range(4)]
         else:
             srcs = [own] + [T.X[j] for j in range(4) if j != c - 4]
-        g.wait_ge(sem.xa, (16 // NP) * (4 if own is None else 3))
+        g.wait_ge(sem.xa, 4 * (4 if own is None else 3))
         call([RemoteDMATransfer(dst_ids=[dst(peer)], dma_engine_mask=0x00FF, remote_sem=sem.pp,
                                 srcs=srcs, dsts=[T.P[:]], alu_op=1)], 8)
         if between is not None:
@@ -61,16 +61,16 @@ def rank_program(g, core, T, topo):
     if rank is not None:
         k = c - 4
         partner = T.cores[(rank + 8) % 16]
-        total = sum(16 if rc < 4 else 8 for rc in RED)
+        total = 16 + 16 + 8 + 8
         g.sync.dma_start(T.S[:], T.x[:]).then_inc(sem.ld, 16)
         g.sync.dma_start(T.y2[:], T.x[:]).then_inc(sem.c2, 16)
         g.wait_ge(sem.ld, 16)
-        tr = [RemoteDMATransfer(dst_ids=[dst(base + rc)], dma_engine_mask=group(p, 16 // NP, 0), remote_sem=sem.xa,
+        tr = [RemoteDMATransfer(dst_ids=[dst(base + rc)], dma_engine_mask=group(p, 4), remote_sem=sem.xa,
                                 src=T.S[p], dst=T.X[k]) for p, rc in enumerate(RED) if rc != c]
-        call(tr, (16 // NP) * len(tr))
+        call(tr, 4 * len(tr))
 
         def send_y2():
-            call([RemoteDMATransfer(dst_ids=[dst(partner)], dma_engine_mask=group(p, 8 // NP, 0), remote_sem=sem.pa,
+            call([RemoteDMATransfer(dst_ids=[dst(partner)], dma_engine_mask=group(p, 2), remote_sem=sem.pa,
                                     src=T.S[p], dst=T.L2[p]) for p in range(NP)], 8)
 
         g.sync.wait_ge(sem.ta, total)

from concourse.bass import DstId, RemoteDMATransfer
from concourse.mybir import AluOpType

RED = [2, 3, 6, 7]
NP = 4
W = 32
SCRATCH = {
    "S": ("dram", [NP, 128, W], "float32"),
    "X": ("dram", [4, 128, W], "float32"),
    "P": ("dram", [128, W], "float32"),
    "L1": ("dram", [NP, 128, W], "float32"),
    "L2": ("dram", [NP, 128, W], "float32"),
}
SEMAPHORES = ["ld", "c2", "st", "a2", "snt", "xa", "pp", "ta", "pa"]


def group(p, n):
    return ((1 << n) - 1) << (p * n)


def rank_program(g, core, T, topo):
    c = core % 8
    if topo.chip(core) > 1:
        return
    base = core - c
    sem = T.sem
    sent = [0]

    def dst(d):
        rid, pid = topo.addr(d, core)
        return DstId(rid=rid, pnc=pid)

    def call(transfers, engines):
        g.remote_dma_fused(transfers, local_sem=sem.snt)
        sent[0] += engines

    def reduce_piece(p, own, between):
        peer = core ^ 8
        if own is None:
            srcs = [T.X[j] for j in range(4)]
        else:
            srcs = [own] + [T.X[j] for j in range(4) if j != c - 4]
        g.wait_ge(sem.xa, 4 * (4 if own is None else 3))
        call([RemoteDMATransfer(dst_ids=[dst(peer)], dma_engine_mask=0x00FF, remote_sem=sem.pp,
                                srcs=srcs, dsts=[T.P[:]], alu_op=1)], 8)
        if between is not None:
            between()
        g.wait_ge(sem.pp, 8)
        srcs = srcs + [T.P[:]]
        if own is None:
            call([RemoteDMATransfer(dst_ids=[dst(base + 4 + j) for j in range(4)], dma_engine_mask=0xFFFF,
                                    remote_sem=sem.ta, srcs=srcs, dsts=[T.L1[p]] * 4, alu_op=1)], 16)
        else:
            others = [base + 4 + j for j in range(4) if j != c - 4]
            call([RemoteDMATransfer(dst_ids=[dst(d) for d in others], dma_engine_mask=0xFF00,
                                    remote_sem=sem.ta, srcs=srcs, dsts=[T.L1[p]] * 3, alu_op=1),
                  RemoteDMATransfer(dst_ids=[dst(peer)], dma_engine_mask=0x00FF,
                                    remote_sem=sem.ta, srcs=srcs, dsts=[T.L1[p]], alu_op=1)], 16)

    rank = T.rank_of(core)
    if rank is not None:
        k = c - 4
        partner = T.cores[(rank + 8) % 16]
        total = 16 + 16 + 8 + 8
        g.sync.dma_start(T.S[:], T.x[:]).then_inc(sem.ld, 16)
        g.sync.dma_start(T.y2[:], T.x[:]).then_inc(sem.c2, 16)
        g.wait_ge(sem.ld, 16)
        tr = [RemoteDMATransfer(dst_ids=[dst(base + rc)], dma_engine_mask=group(p, 4), remote_sem=sem.xa,
                                src=T.S[p], dst=T.X[k]) for p, rc in enumerate(RED) if rc != c]
        call(tr, 4 * len(tr))

        def send_y2():
            call([RemoteDMATransfer(dst_ids=[dst(partner)], dma_engine_mask=group(p, 2), remote_sem=sem.pa,
                                    src=T.S[p], dst=T.L2[p]) for p in range(NP)], 8)

        g.sync.wait_ge(sem.ta, total)
        g.sync.dma_start(T.y1[:], T.L1[:]).then_inc(sem.st, 16)
        if c in RED:
            reduce_piece(RED.index(c), T.S[RED.index(c)], send_y2)
        else:
            send_y2()
        g.wait_ge(sem.pa, 8)
        g.wait_ge(sem.c2, 16)
        g.dma_start(T.y2[:], T.L2[:], accum_op=AluOpType.add, max_dma_last_dim=8192).then_inc(sem.a2, 16)
        g.wait_ge(sem.snt, sent[0])
        g.wait_ge(sem.a2, 16)
        g.wait_ge(sem.ta, total)
        g.wait_ge(sem.st, 16)
        return

    if c in RED:
        reduce_piece(RED.index(c), None, None)
        g.wait_ge(sem.snt, sent[0])
